import numpy as np
CORES = [4,12,20,28,44,60,76,84,92,108,116,124]
N = 12
PG, W, NP = 32, 64, 32
CAPP = 8
def entries(a): return a.T.reshape(-1)
def pack(v, P): return np.ascontiguousarray(np.asarray(v, np.int32).reshape(-1, P).T)
def lists(rng, how):
    I = rng.integers(0, N * PG, (N, NP))
    if how == "alike": I[:] = rng.integers(0, N * PG, (N, 1))
    if how == "hotrank": I = PG * int(rng.integers(N)) + rng.integers(0, PG, (N, NP))
    if how == "own": I = PG * np.arange(N).reshape(N, 1) + rng.integers(0, PG, (N, NP))
    if how == "edge": I = PG * rng.integers(0, N, (N, NP)) + np.where(rng.random((N, NP)) < 0.5, 0, PG - 1)
    if how == "swap": s = int(rng.integers(1, N)); I = np.stack([PG * ((r + s) % N) + np.concatenate([rng.permutation(PG), rng.integers(0, PG, NP)])[:NP] for r in range(N)])
    O = np.stack([rng.permutation(np.repeat(rng.permutation(N)[:NP // CAPP], CAPP)) if how == "full" else rng.permutation(np.repeat(np.arange(N), CAPP))[:NP] for r in range(N)])
    I = PG * O + I % PG
    if how == "full": I = PG * O + np.stack([np.array([np.sum(O[r, :i] == O[r, i]) for i in range(NP)]) for r in range(N)]) % PG
    if how == "sorted": I = np.sort(I, axis=1)
    return {"pt": np.stack([pack(I[r], 16) for r in range(N)])}
def setup_inputs(rng):
    return dict({"pool": rng.standard_normal((N, PG * 128, W), dtype=np.float32)}, **lists(rng, "uniform"))
def setup_inputs_alike(rng):
    d = setup_inputs(rng); d.update(lists(rng, "alike"))
    for k in ("pool",): d[k] = (d[k].astype(np.float32) * 1048576.0).astype(d[k].dtype)
    return d
def setup_inputs_edge(rng):
    d = setup_inputs(rng); d.update(lists(rng, "edge"))
    for k in ("pool",): d[k] = (d[k].astype(np.float32) * (1 / 1024.0)).astype(d[k].dtype)
    return d
def setup_inputs_full(rng):
    d = setup_inputs(rng); d.update(lists(rng, "full"))
    return d
def setup_inputs_sorted(rng):
    d = setup_inputs(rng); d.update(lists(rng, "sorted"))
    return d
def check_inputs(x):
    bad = []
    if x["pt"].min() < 0 or x["pt"].max() >= N * PG: bad.append("pt out of range")
    if max(int(np.bincount(entries(a) // PG, minlength=N).max()) for a in x["pt"]) > CAPP: bad.append("more than CAPP entries of a list point into one rank's part")
    return bad
def reference(pool, pt):
    A = np.concatenate(list(pool), axis=0).reshape(N * PG, 128, W)
    return {"y": np.stack([A[entries(pt[r])].reshape(NP * 128, W) for r in range(N)])}

@@ -1,0 +1,308 @@
+from concourse.bass import DstId, RemoteDMATransfer, IndirectOffsetOnAxis
+from concourse.mybir import AluOpType, AxisListType
+
+NPG = 32
+CAP = 8
+RPP = 16
+TW = 512
+BLK = 128
+POOLR = NPG * RPP
+NSV = 4
+MAXD = 4
+
+SCRATCH = {
+    "tab": ("dram", [POOLR + 11 * BLK, TW], "float32"),
+    "ptab": ("dram", [POOLR, TW], "float32"),
+    "mylist": ("dram", [128, 2], "int32"),
+    "fwd": ("dram", [128, 2], "int32"),
+    "lists": ("dram", [MAXD, 128, 2], "int32"),
+    "tile": ("sbuf", [128, MAXD * TW], "float32"),
+    "zr": ("sbuf", [128, 224], "int32"),
+    "lrow": ("sbuf", [128, 128], "int32"),
+    "lb": ("sbuf", [128, 128], "int32"),
+    "cm": ("sbuf", [128, 128], "int32"),
+    "own": ("sbuf", [128, 128], "int32"),
+    "ma": ("sbuf", [128, 128], "float32"),
+    "mb": ("sbuf", [128, 128], "float32"),
+    "w0": ("sbuf", [128, 128], "float32"),
+    "w1": ("sbuf", [128, 128], "float32"),
+    "w2": ("sbuf", [128, 128], "float32"),
+    "w3": ("sbuf", [128, 128], "float32"),
+    "ki": ("sbuf", [128, 16], "int32"),
+    "kf": ("sbuf", [128, 40], "float32"),
+    "idx": ("sbuf", [128, 4], "int32"),
+}
+SEMAPHORES = ["ms", "ps", "gl", "gs0", "gs1", "gs2", "gs3", "gi", "gb", "v", "fs", "ls", "rs", "arr", "sent", "st", "zs"]
+
+
+def _bits(mask):
+    return [b for b in range(mask.bit_length()) if (mask >> b) & 1]
+
+
+def _mask(bits):
+    m = 0
+    for b in bits:
+        m |= 1 << b
+    return m
+
+
+def _plan(cores, topo):
+    n = len(cores)
+    allc = range(topo.CHIPS * topo.CORES_PER_CHIP)
+    chips = [topo.chip(c) for c in cores]
+    mate = {}
+    for a in range(topo.CHIPS):
+        for b in range(topo.CHIPS):
+            if topo.mates(a, b):
+                mate[a] = b
+    sv = []
+    for i, rc in enumerate(cores):
+        probe = [c for c in allc if topo.chip(c) == mate[chips[i]]][0]
+        ownr = [c for c in allc if topo.chip(c) == chips[i] and c != rc and topo.may_write(c, probe)]
+        near = [c for c in ownr if topo.die(c) == topo.die(rc)]
+        far = [c for c in ownr if topo.die(c) != topo.die(rc)]
+        sv.append([near[0], far[0], near[1], far[1]])
+
+    def links(a, b, d):
+        if topo.same_plane(a, b):
+            return [("out", a, d), ("in", b, d)]
+        if topo.mates(a, b):
+            return [("mate", a, d)]
+        return [("mate", a, d), ("out", mate[a], d), ("in", b, d)]
+
+    load = {}
+    side = {}
+    for k in range(1, n):
+        for s in range(n):
+            r = (s + k) % n
+            best = None
+            for h in (0, 1):
+                d = topo.die(sv[s][h])
+                ls = links(chips[s], chips[r], d) + [("src", s, d)]
+                key = (max(load.get(x, 0) for x in ls), sum(load.get(x, 0) for x in ls), h)
+                if best is None or key < best[0]:
+                    best = (key, h, ls)
+            for x in best[2]:
+                load[x] = load.get(x, 0) + 1
+            side[(s, r)] = best[1]
+    serve = [[[] for h in range(NSV)] for s in range(n)]
+    where = {}
+    for s in range(n):
+        for h in (0, 1):
+            ds = [(s + k) % n for k in range(1, n) if side[(s, (s + k) % n)] == h]
+            late = len(ds) // 3
+            serve[s][h] = ds[:len(ds) - late]
+            serve[s][2 + h] = ds[len(ds) - late:]
+        for h in range(NSV):
+            for a, r in enumerate(serve[s][h]):
+                where[(s, r)] = (sv[s][h], a)
+    passon = [[[where[(s, r)] for s in [x for x in range(n) if x != r][h::NSV]] for h in range(NSV)] for r in range(n)]
+    return sv, serve, where, passon
+
+
+def _common_mask(topo, src, dsts):
+    m = topo.mask(src, dsts[0])
+    for d in dsts[1:]:
+        m &= topo.mask(src, d)
+    return m
+
+
+def _dst(topo, c):
+    rid, pid, _se = topo.addr(c)
+    return DstId(rid=rid, pnc=pid)
+
+
+def rank_program(g, core, T, topo):
+    cores = list(T.cores)
+    n = len(cores)
+    sv, serve, where, passon = _plan(cores, topo)
+    S = T.sem
+    A = AluOpType
+    vec = g.vector
+    nv = [0]
+
+    def bar():
+        if nv[0]:
+            vec.wait_ge(S.v, nv[0])
+
+    def op(ins):
+        ins.then_inc(S.v, 1)
+        nv[0] += 1
+
+    def partition_consts():
+        vec.wait_ge(S.gi, 2)
+        op(vec.tensor_scalar(T.ki[:, 1:2], T.ki[:, 0:1], 4, None, op0=A.arith_shift_right))
+        op(vec.tensor_scalar(T.ki[:, 2:3], T.ki[:, 0:1], 15, None, op0=A.bitwise_and))
+        bar()
+        op(vec.tensor_scalar(T.kf[:, 0:1], T.ki[:, 1:2], 1.0, None, op0=A.add))
+        op(vec.tensor_copy(T.kf[:, 1:2], T.ki[:, 2:3]))
+        op(vec.tensor_scalar(T.kf[:, 2:3], T.ki[:, 1:2], 2.0, None, op0=A.mult))
+
+    gs = [S.gs0, S.gs1, S.gs2, S.gs3]
+    rank = T.rank_of(core)
+
+    if rank is not None:
+        mine = sv[rank]
+        sent = 0
+        g.dma_start(T.lrow[0:1, 0:NPG], T.pt[:, :]).then_inc(S.gl, 16)
+        g.sync.dma_start(T.mylist[0:16, :], T.pt[:, :]).then_inc(S.ms, 16)
+        vec.memset(T.zr[0:1, :], 0).then_inc(S.zs, 1)
+        g.scalar.wait_ge(S.zs, 1)
+        g.scalar.dma_start(T.mylist[16:128, :], T.zr[0:1, :]).then_inc(S.ms, 16)
+        for q in range(4):
+            eng = g.scalar if q % 2 == 0 else g.sync
+            eng.dma_start(T.tab[BLK * q:BLK * (q + 1), :], T.pool[1024 * q:1024 * (q + 1), :]).then_inc(S.ps, 16)
+        g.iota(T.ki[:, 0:1], [[0, 1]], 0, 1).then_inc(S.gi, 1)
+        g.iota(T.cm[:, :], [[-1, 2], [-16, 2], [1, NPG]], 0, 0).then_inc(S.gi, 1)
+
+        g.wait_ge(S.ms, 32)
+        lm = _mask(_bits(_common_mask(topo, core, mine))[:1])
+        g.remote_dma_fused([RemoteDMATransfer(dst_ids=[_dst(topo, c) for c in mine], dma_engine_mask=lm, remote_sem=S.fs,
+                                              srcs=[T.mylist[:, :]], dsts=[T.fwd[:, :] for c in mine], alu_op=0)],
+                           local_sem=S.sent)
+        sent += 1
+        g.wait_ge(S.ps, 64)
+        for pair in (mine[0:2], mine[2:4]):
+            eb = _bits(_common_mask(topo, core, pair))
+            per = len(eb) // 8
+            trs = []
+            for q in range(4):
+                for w, c in enumerate(pair):
+                    mk = _mask(eb[2 * per * q + w:2 * per * (q + 1):2])
+                    trs.append(RemoteDMATransfer(dst_ids=[_dst(topo, c)], dma_engine_mask=mk, remote_sem=S.rs,
+                                                 src=T.tab[BLK * q:BLK * (q + 1), :], dst=T.ptab[BLK * q:BLK * (q + 1), :]))
+                    sent += per
+            g.remote_dma_fused(trs, local_sem=S.sent)
+        g.wait_ge(S.gl, 16)
+        g.partition_broadcast(T.lb[:, 0:NPG], T.lrow[0:1, 0:NPG], 128).then_inc(S.gb, 1)
+
+        partition_consts()
+        bar()
+        op(vec.tensor_scalar(T.ma[:, :], T.cm[:, :], T.kf[:, 2:3], 0.0, op0=A.subtract, op1=A.is_equal))
+        op(vec.tensor_scalar(T.mb[:, :], T.cm[:, :], T.kf[:, 2:3], 0.0, op0=A.subtract, op1=A.is_lt))
+        vec.wait_ge(S.gb, 1)
+        op(vec.tensor_copy(T.w0[:, 0:NPG], T.lb[:, 0:NPG]))
+        op(vec.tensor_scalar(T.own[:, 0:NPG], T.lb[:, 0:NPG], 5, None, op0=A.arith_shift_right))
+        bar()
+        op(vec.tensor_copy(T.w1[:, 0:NPG], T.own[:, 0:NPG]))
+        for t in range(4):
+            op(vec.tensor_tensor(T.w2[:, NPG * t:NPG * (t + 1)], T.ma[:, NPG * t:NPG * (t + 1)], T.w0[:, 0:NPG], A.mult))
+        bar()
+        for t in range(4):
+            op(vec.tensor_reduce(T.kf[:, 4 + t:5 + t], T.w2[:, NPG * t:NPG * (t + 1)], AxisListType.X, A.add))
+        bar()
+        op(vec.tensor_copy(T.ki[:, 4:8], T.kf[:, 4:8]))
+        bar()
+        op(vec.tensor_scalar(T.ki[:, 8:12], T.ki[:, 4:8], 5, None, op0=A.arith_shift_right))
+        op(vec.tensor_scalar(T.ki[:, 12:16], T.ki[:, 4:8], NPG - 1, None, op0=A.bitwise_and))
+        bar()
+        op(vec.tensor_copy(T.kf[:, 8:12], T.ki[:, 8:12]))
+        op(vec.tensor_scalar(T.kf[:, 12:16], T.ki[:, 12:16], float(RPP), None, op0=A.mult))
+        bar()
+        for t in range(4):
+            op(vec.tensor_scalar(T.w3[:, NPG * t:NPG * (t + 1)], T.w1[:, 0:NPG], T.kf[:, 8 + t:9 + t], None, op0=A.is_equal))
+        op(vec.tensor_scalar(T.kf[:, 16:20], T.kf[:, 8:12], float(BLK), float(POOLR), op0=A.mult, op1=A.add))
+        op(vec.tensor_scalar(T.kf[:, 20:24], T.kf[:, 8:12], float(rank), None, op0=A.is_equal))
+        op(vec.tensor_scalar(T.kf[:, 32:36], T.kf[:, 8:12], float(rank), float(BLK), op0=A.is_gt, op1=A.mult))
+        bar()
+        op(vec.tensor_tensor(T.w2[:, :], T.w3[:, :], T.mb[:, :], A.mult))
+        bar()
+        for t in range(4):
+            op(vec.tensor_reduce(T.kf[:, 24 + t:25 + t], T.w2[:, NPG * t:NPG * (t + 1)], AxisListType.X, A.add))
+        bar()
+        op(vec.tensor_scalar(T.kf[:, 28:32], T.kf[:, 24:28], float(RPP), None, op0=A.mult))
+        op(vec.tensor_tensor(T.kf[:, 16:20], T.kf[:, 16:20], T.kf[:, 32:36], A.subtract))
+        bar()
+        op(vec.tensor_tensor(T.kf[:, 16:20], T.kf[:, 16:20], T.kf[:, 28:32], A.add))
+        bar()
+        op(vec.tensor_tensor(T.kf[:, 12:16], T.kf[:, 12:16], T.kf[:, 16:20], A.subtract))
+        bar()
+        op(vec.tensor_tensor(T.kf[:, 12:16], T.kf[:, 12:16], T.kf[:, 20:24], A.mult))
+        bar()
+        op(vec.tensor_tensor(T.kf[:, 16:20], T.kf[:, 16:20], T.kf[:, 12:16], A.add))
+        bar()
+        op(vec.tensor_scalar(T.idx[:, 0:4], T.kf[:, 16:20], T.kf[:, 1:2], None, op0=A.add))
+
+        g.wait_ge(S.v, nv[0])
+        need = 0
+        for s in range(n):
+            if s != rank:
+                need += len(_bits(topo.mask(where[(s, rank)][0], core)))
+        g.wait_ge(S.arr, need)
+        rows = T.tab.shape[0]
+        for t in range(4):
+            g.indirect_dma_start(T.tile[:, TW * t:TW * (t + 1)], None, T.tab[:],
+                                 IndirectOffsetOnAxis(ap=T.idx[:, t:t + 1], axis=0), bounds_check=rows - 1).then_inc(gs[t], 16)
+        for t in range(4):
+            eng = g.sync if t % 2 == 0 else g.scalar
+            eng.wait_ge(gs[t], 16)
+            eng.dma_start(T.y[1024 * t:1024 * (t + 1), :], T.tile[:, TW * t:TW * (t + 1)]).then_inc(S.st, 16)
+        g.wait_ge(S.sent, sent)
+        g.wait_ge(S.st, 64)
+        return
+
+    who = [(s, h) for s in range(n) for h in range(NSV) if sv[s][h] == core]
+    if not who:
+        return
+    s, h = who[0]
+    askers = serve[s][h]
+    m = len(askers)
+    F = NPG * m
+    sent = 0
+    g.iota(T.ki[:, 0:1], [[0, 1]], 0, 1).then_inc(S.gi, 1)
+    g.iota(T.cm[:, 0:F], [[0, m], [1, NPG]], 0, 0).then_inc(S.gi, 1)
+
+    tg = passon[s][h]
+    fm = _common_mask(topo, core, [c for c, a in tg])
+    g.wait_ge(S.fs, 1)
+    g.remote_dma_fused([RemoteDMATransfer(dst_ids=[_dst(topo, c) for c, a in tg], dma_engine_mask=fm, remote_sem=S.ls,
+                                          srcs=[T.fwd[:, :]], dsts=[T.lists[a] for c, a in tg], alu_op=0)],
+                       local_sem=S.sent)
+    sent += len(_bits(fm))
+
+    need = 0
+    for r in askers:
+        for hh in range(NSV):
+            if (core, askers.index(r)) in passon[r][hh]:
+                need += len(_bits(_common_mask(topo, sv[r][hh], [c for c, a in passon[r][hh]])))
+    g.wait_ge(S.ls, need)
+    g.dma_start(T.lrow[0:1, 0:F], T.lists[0:m, 0:16, :]).then_inc(S.gl, 16)
+    g.wait_ge(S.gl, 16)
+    g.partition_broadcast(T.lb[:, 0:F], T.lrow[0:1, 0:F], 128).then_inc(S.gb, 1)
+
+    partition_consts()
+    op(vec.tensor_scalar(T.ma[:, 0:F], T.cm[:, 0:F], 0.0, None, op0=A.is_gt))
+    vec.wait_ge(S.gb, 1)
+    op(vec.tensor_scalar(T.own[:, 0:F], T.lb[:, 0:F], 5, None, op0=A.arith_shift_right))
+    op(vec.tensor_scalar(T.w3[:, 0:F], T.lb[:, 0:F], float(NPG * s), float(RPP), op0=A.subtract, op1=A.mult))
+    bar()
+    op(vec.tensor_scalar(T.w0[:, 0:F], T.own[:, 0:F], float(s), None, op0=A.is_equal))
+    bar()
+    op(vec.tensor_tensor_scan(T.w1[:, 0:F], T.ma[:, 0:F], T.w0[:, 0:F], 0.0, A.mult, A.add))
+    bar()
+    op(vec.tensor_tensor(T.w2[:, 0:F], T.w1[:, 0:F], T.w0[:, 0:F], A.mult))
+    bar()
+    op(vec.tensor_scalar(T.w1[:, 0:F], T.w2[:, 0:F], T.kf[:, 0:1], None, op0=A.is_equal))
+    bar()
+    op(vec.tensor_tensor(T.w2[:, 0:F], T.w1[:, 0:F], T.w3[:, 0:F], A.mult))
+    bar()
+    for a in range(m):
+        op(vec.tensor_reduce(T.kf[:, 4 + a:5 + a], T.w2[:, NPG * a:NPG * (a + 1)], AxisListType.X, A.add))
+    bar()
+    op(vec.tensor_scalar(T.idx[:, 0:m], T.kf[:, 4:4 + m], T.kf[:, 1:2], None, op0=A.add))
+
+    g.wait_ge(S.v, nv[0])
+    pair = sv[s][0:2] if h < 2 else sv[s][2:4]
+    g.wait_ge(S.rs, 4 * (len(_bits(_common_mask(topo, cores[s], pair))) // 8))
+    for a in range(m):
+        g.indirect_dma_start(T.tile[:, TW * a:TW * (a + 1)], None, T.ptab[:],
+                             IndirectOffsetOnAxis(ap=T.idx[:, a:a + 1], axis=0), bounds_check=POOLR - 1).then_inc(gs[a], 16)
+    for a, r in enumerate(askers):
+        base = POOLR + BLK * (s if s < r else s - 1)
+        dst = cores[r]
+        rid, pid, _se = topo.addr(dst)
+        mk = topo.mask(core, dst)
+        g.wait_ge(gs[a], 16)
+        g.remote_dma(T.tab[base:base + BLK, :], T.tile[:, TW * a:TW * (a + 1)], S.arr, S.sent, pid, rid, mk)
+        sent += len(_bits(mk))
+    g.wait_ge(S.sent, sent)

@@ -19,6 +19,9 @@ SCRATCH = {
     "tile": ("sbuf", [128, MAXD * TW], "float32"),
     "zr": ("sbuf", [128, 224], "int32"),
     "lrow": ("sbuf", [128, 128], "int32"),
+    "lrf": ("sbuf", [128, 128], "float32"),
+    "ones": ("sbuf", [128, 128], "float32"),
+    "pb": ("psum", [128, 128], "float32"),
     "lb": ("sbuf", [128, 128], "int32"),
     "cm": ("sbuf", [128, 128], "int32"),
     "own": ("sbuf", [128, 128], "int32"),
@@ -28,11 +31,14 @@ SCRATCH = {
     "w1": ("sbuf", [128, 128], "float32"),
     "w2": ("sbuf", [128, 128], "float32"),
     "w3": ("sbuf", [128, 128], "float32"),
+    "w4": ("sbuf", [128, 128], "float32"),
+    "w5": ("sbuf", [128, 128], "float32"),
     "ki": ("sbuf", [128, 16], "int32"),
     "kf": ("sbuf", [128, 40], "float32"),
     "idx": ("sbuf", [128, 4], "int32"),
 }
-SEMAPHORES = ["ms", "ps", "gl", "gs0", "gs1", "gs2", "gs3", "gi", "gb", "v", "fs", "ls", "rs", "arr", "sent", "st", "zs"]
+SEMAPHORES = ["ms", "psa", "psb", "gl", "sl", "mm", "gs0", "gs1", "gs2", "gs3", "gi", "gb", "v", "fs", "ls",
+              "rsa", "rsb", "rs", "arr", "sent", "st", "zs"]
 
 
 def _bits(mask):
@@ -90,14 +96,17 @@ def _plan(cores, topo):
     for s in range(n):
         for h in (0, 1):
             ds = [(s + k) % n for k in range(1, n) if side[(s, (s + k) % n)] == h]
-            late = len(ds) // 3
+            ds.sort(key=lambda r: 0 if topo.may_write(cores[r], sv[s][h]) else 1)
+            late = len(ds) // 2
             serve[s][h] = ds[:len(ds) - late]
             serve[s][2 + h] = ds[len(ds) - late:]
         for h in range(NSV):
             for a, r in enumerate(serve[s][h]):
                 where[(s, r)] = (sv[s][h], a)
-    passon = [[[where[(s, r)] for s in [x for x in range(n) if x != r][h::NSV]] for h in range(NSV)] for r in range(n)]
-    return sv, serve, where, passon
+    direct = [[where[(s, r)] for s in range(n) if s != r and topo.may_write(cores[r], where[(s, r)][0])] for r in range(n)]
+    passon = [[[where[(s, r)] for s in [x for x in range(n) if x != r and not topo.may_write(cores[r], where[(x, r)][0])][h::NSV]]
+               for h in range(NSV)] for r in range(n)]
+    return sv, serve, where, passon, direct
 
 
 def _common_mask(topo, src, dsts):
@@ -115,7 +124,7 @@ def _dst(topo, c):
 def rank_program(g, core, T, topo):
     cores = list(T.cores)
     n = len(cores)
-    sv, serve, where, passon = _plan(cores, topo)
+    sv, serve, where, passon, direct = _plan(cores, topo)
     S = T.sem
     A = AluOpType
     vec = g.vector
@@ -144,35 +153,43 @@ def rank_program(g, core, T, topo):
     if rank is not None:
         mine = sv[rank]
         sent = 0
-        g.dma_start(T.lrow[0:1, 0:NPG], T.pt[:, :]).then_inc(S.gl, 16)
         g.sync.dma_start(T.mylist[0:16, :], T.pt[:, :]).then_inc(S.ms, 16)
         vec.memset(T.zr[0:1, :], 0).then_inc(S.zs, 1)
         g.scalar.wait_ge(S.zs, 1)
         g.scalar.dma_start(T.mylist[16:128, :], T.zr[0:1, :]).then_inc(S.ms, 16)
         for q in range(4):
             eng = g.scalar if q % 2 == 0 else g.sync
-            eng.dma_start(T.tab[BLK * q:BLK * (q + 1), :], T.pool[1024 * q:1024 * (q + 1), :]).then_inc(S.ps, 16)
-        g.iota(T.ki[:, 0:1], [[0, 1]], 0, 1).then_inc(S.gi, 1)
-        g.iota(T.cm[:, :], [[-1, 2], [-16, 2], [1, NPG]], 0, 0).then_inc(S.gi, 1)
+            eng.dma_start(T.tab[BLK * q:BLK * (q + 1), :], T.pool[1024 * q:1024 * (q + 1), :]).then_inc(S.psa if q < 2 else S.psb, 16)
 
         g.wait_ge(S.ms, 32)
-        lm = _mask(_bits(_common_mask(topo, core, mine))[:1])
+        dg = direct[rank]
+        lm = _mask(_bits(_common_mask(topo, core, mine + [c for c, a in dg]))[:1])
         g.remote_dma_fused([RemoteDMATransfer(dst_ids=[_dst(topo, c) for c in mine], dma_engine_mask=lm, remote_sem=S.fs,
                                               srcs=[T.mylist[:, :]], dsts=[T.fwd[:, :] for c in mine], alu_op=0)],
                            local_sem=S.sent)
         sent += 1
-        g.wait_ge(S.ps, 64)
-        for pair in (mine[0:2], mine[2:4]):
-            eb = _bits(_common_mask(topo, core, pair))
-            per = len(eb) // 8
+        g.remote_dma_fused([RemoteDMATransfer(dst_ids=[_dst(topo, c) for c, a in dg], dma_engine_mask=lm, remote_sem=S.ls,
+                                              srcs=[T.mylist[:, :]], dsts=[T.lists[a] for c, a in dg], alu_op=0)],
+                           local_sem=S.sent)
+        sent += 1
+        pair = mine[0:2]
+        eb = _bits(_common_mask(topo, core, pair))
+        per = len(eb) // 4
+        for half, (lsem, rsem) in enumerate(((S.psa, S.rsa), (S.psb, S.rsb))):
+            g.wait_ge(lsem, 32)
             trs = []
-            for q in range(4):
+            for qi in range(2):
+                q = 2 * half + qi
                 for w, c in enumerate(pair):
-                    mk = _mask(eb[2 * per * q + w:2 * per * (q + 1):2])
-                    trs.append(RemoteDMATransfer(dst_ids=[_dst(topo, c)], dma_engine_mask=mk, remote_sem=S.rs,
+                    mk = _mask(eb[2 * per * qi + w:2 * per * (qi + 1):2])
+                    trs.append(RemoteDMATransfer(dst_ids=[_dst(topo, c)], dma_engine_mask=mk, remote_sem=rsem,
                                                  src=T.tab[BLK * q:BLK * (q + 1), :], dst=T.ptab[BLK * q:BLK * (q + 1), :]))
                     sent += per
             g.remote_dma_fused(trs, local_sem=S.sent)
+
+        g.dma_start(T.lrow[0:1, 0:NPG], T.pt[:, :]).then_inc(S.gl, 16)
+        g.iota(T.ki[:, 0:1], [[0, 1]], 0, 1).then_inc(S.gi, 1)
+        g.iota(T.cm[:, :], [[-1, 2], [-16, 2], [1, NPG]], 0, 0).then_inc(S.gi, 1)
         g.wait_ge(S.gl, 16)
         g.partition_broadcast(T.lb[:, 0:NPG], T.lrow[0:1, 0:NPG], 128).then_inc(S.gb, 1)
 
@@ -260,31 +277,52 @@ def rank_program(g, core, T, topo):
                        local_sem=S.sent)
     sent += len(_bits(fm))
 
+    pe = _bits(topo.mask(sv[s][h % 2], sv[s][2 + h % 2]))
+    hp = len(pe) // 2
+    if h < 2:
+        rper = len(_bits(_common_mask(topo, cores[s], sv[s][0:2]))) // 4
+        for half, rsem in enumerate((S.rsa, S.rsb)):
+            g.wait_ge(rsem, 2 * rper)
+            trs = []
+            for qi in range(2):
+                q = 2 * half + qi
+                trs.append(RemoteDMATransfer(dst_ids=[_dst(topo, sv[s][2 + h])], dma_engine_mask=_mask(pe[hp * qi:hp * (qi + 1)]),
+                                             remote_sem=S.rs, src=T.ptab[BLK * q:BLK * (q + 1), :],
+                                             dst=T.ptab[BLK * q:BLK * (q + 1), :]))
+                sent += hp
+            g.remote_dma_fused(trs, local_sem=S.sent)
+
     need = 0
     for r in askers:
+        if (core, askers.index(r)) in direct[r]:
+            need += 1
         for hh in range(NSV):
             if (core, askers.index(r)) in passon[r][hh]:
                 need += len(_bits(_common_mask(topo, sv[r][hh], [c for c, a in passon[r][hh]])))
-    g.wait_ge(S.ls, need)
-    g.dma_start(T.lrow[0:1, 0:F], T.lists[0:m, 0:16, :]).then_inc(S.gl, 16)
-    g.wait_ge(S.gl, 16)
-    g.partition_broadcast(T.lb[:, 0:F], T.lrow[0:1, 0:F], 128).then_inc(S.gb, 1)
+    g.sync.wait_ge(S.ls, need)
+    g.sync.dma_start(T.lrow[0:1, 0:F], T.lists[0:m, 0:16, :]).then_inc(S.sl, 16)
 
+    op(vec.memset(T.ones[0:1, :], 1.0))
     partition_consts()
     op(vec.tensor_scalar(T.ma[:, 0:F], T.cm[:, 0:F], 0.0, None, op0=A.is_gt))
-    vec.wait_ge(S.gb, 1)
-    op(vec.tensor_scalar(T.own[:, 0:F], T.lb[:, 0:F], 5, None, op0=A.arith_shift_right))
-    op(vec.tensor_scalar(T.w3[:, 0:F], T.lb[:, 0:F], float(NPG * s), float(RPP), op0=A.subtract, op1=A.mult))
+    vec.wait_ge(S.sl, 16)
+    op(vec.tensor_copy(T.lrf[0:1, 0:F], T.lrow[0:1, 0:F]))
+    g.tensor.wait_ge(S.v, nv[0])
+    g.tensor.matmul(T.pb[:, 0:F], T.ones[0:1, :], T.lrf[0:1, 0:F], True, True).then_inc(S.mm, 1)
+    vec.wait_ge(S.mm, 1)
     bar()
-    op(vec.tensor_scalar(T.w0[:, 0:F], T.own[:, 0:F], float(s), None, op0=A.is_equal))
+    lo = float(NPG * s)
+    op(vec.tensor_scalar(T.w4[:, 0:F], T.pb[:, 0:F], lo, lo + float(NPG - 1), op0=A.max, op1=A.min))
+    op(vec.tensor_scalar(T.w3[:, 0:F], T.pb[:, 0:F], lo, float(RPP), op0=A.subtract, op1=A.mult))
+    bar()
+    op(vec.tensor_tensor(T.w0[:, 0:F], T.w4[:, 0:F], T.pb[:, 0:F], A.is_equal))
     bar()
     op(vec.tensor_tensor_scan(T.w1[:, 0:F], T.ma[:, 0:F], T.w0[:, 0:F], 0.0, A.mult, A.add))
+    op(vec.tensor_tensor(T.w5[:, 0:F], T.w0[:, 0:F], T.w3[:, 0:F], A.mult))
     bar()
-    op(vec.tensor_tensor(T.w2[:, 0:F], T.w1[:, 0:F], T.w0[:, 0:F], A.mult))
+    op(vec.tensor_scalar(T.mb[:, 0:F], T.w1[:, 0:F], T.kf[:, 0:1], None, op0=A.is_equal))
     bar()
-    op(vec.tensor_scalar(T.w1[:, 0:F], T.w2[:, 0:F], T.kf[:, 0:1], None, op0=A.is_equal))
-    bar()
-    op(vec.tensor_tensor(T.w2[:, 0:F], T.w1[:, 0:F], T.w3[:, 0:F], A.mult))
+    op(vec.tensor_tensor(T.w2[:, 0:F], T.mb[:, 0:F], T.w5[:, 0:F], A.mult))
     bar()
     for a in range(m):
         op(vec.tensor_reduce(T.kf[:, 4 + a:5 + a], T.w2[:, NPG * a:NPG * (a + 1)], AxisListType.X, A.add))
@@ -292,17 +330,28 @@ def rank_program(g, core, T, topo):
     op(vec.tensor_scalar(T.idx[:, 0:m], T.kf[:, 4:4 + m], T.kf[:, 1:2], None, op0=A.add))
 
     g.wait_ge(S.v, nv[0])
-    pair = sv[s][0:2] if h < 2 else sv[s][2:4]
-    g.wait_ge(S.rs, 4 * (len(_bits(_common_mask(topo, cores[s], pair))) // 8))
-    for a in range(m):
+    if h >= 2:
+        g.wait_ge(S.rs, 4 * hp)
+
+    def gather(a):
         g.indirect_dma_start(T.tile[:, TW * a:TW * (a + 1)], None, T.ptab[:],
                              IndirectOffsetOnAxis(ap=T.idx[:, a:a + 1], axis=0), bounds_check=POOLR - 1).then_inc(gs[a], 16)
-    for a, r in enumerate(askers):
+
+    def send(a):
+        r = askers[a]
         base = POOLR + BLK * (s if s < r else s - 1)
         dst = cores[r]
         rid, pid, _se = topo.addr(dst)
         mk = topo.mask(core, dst)
         g.wait_ge(gs[a], 16)
         g.remote_dma(T.tab[base:base + BLK, :], T.tile[:, TW * a:TW * (a + 1)], S.arr, S.sent, pid, rid, mk)
-        sent += len(_bits(mk))
+        return len(_bits(mk))
+
+    ahead = 2 if h < 2 else m
+    for a in range(min(ahead, m)):
+        gather(a)
+    for a in range(m):
+        sent += send(a)
+        if a + ahead < m:
+            gather(a + ahead)
     g.wait_ge(S.sent, sent)

@@ -1,29 +1,36 @@
-from concourse.bass import DstId, RemoteDMATransfer, IndirectOffsetOnAxis
-from concourse.mybir import AluOpType, AxisListType
+from concourse.bass import DstId, RemoteDMATransfer
+from concourse.mybir import AluOpType, AxisListType, ActivationFunctionType
 
 NPG = 32
 CAP = 8
+PW = 64
 RPP = 16
-TW = 512
+TW = CAP * PW
 BLK = 128
 POOLR = NPG * RPP
+POOLC = NPG * PW
+OC = 32
 NSV = 4
 MAXD = 4
 
 SCRATCH = {
-    "tab": ("dram", [POOLR + 11 * BLK, TW], "float32"),
-    "ptab": ("dram", [POOLR, TW], "float32"),
+    "win": ("sbuf", [128, POOLC + 11 * TW], "float32"),
+    "tile": ("sbuf", [128, MAXD * TW], "float32"),
     "mylist": ("dram", [128, 2], "int32"),
     "fwd": ("dram", [128, 2], "int32"),
     "lists": ("dram", [MAXD, 128, 2], "int32"),
-    "tile": ("sbuf", [128, MAXD * TW], "float32"),
     "zr": ("sbuf", [128, 224], "int32"),
     "lrow": ("sbuf", [128, 128], "int32"),
     "lrf": ("sbuf", [128, 128], "float32"),
     "ones": ("sbuf", [128, 128], "float32"),
     "pb": ("psum", [128, 128], "float32"),
+    "pb2": ("psum", [128, 128], "float32"),
     "lb": ("sbuf", [128, 128], "int32"),
     "cm": ("sbuf", [128, 128], "int32"),
+    "dm": ("sbuf", [128, OC], "int32"),
+    "dd": ("sbuf", [128, OC], "float32"),
+    "rhs": ("sbuf", [128, 128], "float32"),
+    "off": ("sbuf", [128, 128], "uint16"),
     "own": ("sbuf", [128, 128], "int32"),
     "ma": ("sbuf", [128, 128], "float32"),
     "mb": ("sbuf", [128, 128], "float32"),
@@ -35,7 +42,6 @@ SCRATCH = {
     "w5": ("sbuf", [128, 128], "float32"),
     "ki": ("sbuf", [128, 16], "int32"),
     "kf": ("sbuf", [128, 40], "float32"),
-    "idx": ("sbuf", [128, 4], "int32"),
 }
 SEMAPHORES = ["ms", "psa", "psb", "gl", "sl", "mm", "gs0", "gs1", "gs2", "gs3", "gi", "gb", "v", "fs", "ls",
               "rsa", "rsb", "rs", "arr", "sent", "st", "zs"]
@@ -129,6 +135,7 @@ def rank_program(g, core, T, topo):
     A = AluOpType
     vec = g.vector
     nv = [0]
+    nmm = [0]
 
     def bar():
         if nv[0]:
@@ -138,28 +145,56 @@ def rank_program(g, core, T, topo):
         ins.then_inc(S.v, 1)
         nv[0] += 1
 
+    def iotas():
+        g.iota(T.ki[:, 0:1], [[0, 1]], 0, 1).then_inc(S.gi, 1)
+        g.iota(T.dm[:, :], [[16, CAP], [1, 4]], 0, -1).then_inc(S.gi, 1)
+
     def partition_consts():
-        vec.wait_ge(S.gi, 2)
+        vec.wait_ge(S.gi, 3)
         op(vec.tensor_scalar(T.ki[:, 1:2], T.ki[:, 0:1], 4, None, op0=A.arith_shift_right))
         op(vec.tensor_scalar(T.ki[:, 2:3], T.ki[:, 0:1], 15, None, op0=A.bitwise_and))
+        op(vec.tensor_scalar(T.ki[:, 3:4], T.ki[:, 0:1], 3, None, op0=A.bitwise_and))
+        op(vec.tensor_scalar(T.dd[:, :], T.dm[:, :], 0.0, None, op0=A.is_equal))
         bar()
         op(vec.tensor_scalar(T.kf[:, 0:1], T.ki[:, 1:2], 1.0, None, op0=A.add))
         op(vec.tensor_copy(T.kf[:, 1:2], T.ki[:, 2:3]))
         op(vec.tensor_scalar(T.kf[:, 2:3], T.ki[:, 1:2], 2.0, None, op0=A.mult))
+        op(vec.tensor_scalar(T.kf[:, 3:4], T.ki[:, 3:4], 16.0, None, op0=A.mult))
+
+    def offsets(v0, m):
+        bar()
+        for a in range(m):
+            op(vec.tensor_scalar(T.rhs[:, OC * a:OC * (a + 1)], T.dd[:, :], T.kf[:, v0 + a:v0 + a + 1], None, op0=A.mult))
+        g.tensor.wait_ge(S.v, nv[0])
+        g.tensor.matmul(T.pb2[:, 0:OC * m], T.ones[:, :], T.rhs[:, 0:OC * m], True, True).then_inc(S.mm, 1)
+        nmm[0] += 1
+        vec.wait_ge(S.mm, nmm[0])
+        op(vec.tensor_scalar(T.off[:, 0:OC * m], T.pb2[:, 0:OC * m], T.kf[:, 1:2], None, op0=A.add))
 
     gs = [S.gs0, S.gs1, S.gs2, S.gs3]
+
+    def pick(a, cols):
+        src = T.win[:, 0:cols].indirect(T.off[:, OC * a:OC * (a + 1)])
+        if a % 2 == 0:
+            vec.tensor_copy(T.tile[:, TW * a:TW * (a + 1)], src).then_inc(gs[a], 1)
+        else:
+            g.scalar.activation(T.tile[:, TW * a:TW * (a + 1)], src, ActivationFunctionType.Copy).then_inc(gs[a], 1)
+
     rank = T.rank_of(core)
 
     if rank is not None:
         mine = sv[rank]
         sent = 0
         g.sync.dma_start(T.mylist[0:16, :], T.pt[:, :]).then_inc(S.ms, 16)
+        g.sync.dma_start(T.lrow[0:1, 0:NPG], T.pt[:, :]).then_inc(S.gl, 16)
         vec.memset(T.zr[0:1, :], 0).then_inc(S.zs, 1)
         g.scalar.wait_ge(S.zs, 1)
         g.scalar.dma_start(T.mylist[16:128, :], T.zr[0:1, :]).then_inc(S.ms, 16)
-        for q in range(4):
-            eng = g.scalar if q % 2 == 0 else g.sync
-            eng.dma_start(T.tab[BLK * q:BLK * (q + 1), :], T.pool[1024 * q:1024 * (q + 1), :]).then_inc(S.psa if q < 2 else S.psb, 16)
+        for pg in range(NPG):
+            eng = g.scalar if pg % 2 == 0 else g.sync
+            eng.dma_start(T.win[:, PW * pg:PW * (pg + 1)], T.pool[128 * pg:128 * (pg + 1), :]).then_inc(
+                S.psa if pg < NPG // 2 else S.psb, 16)
+        half_in = 16 * (NPG // 2)
 
         g.wait_ge(S.ms, 32)
         dg = direct[rank]
@@ -176,23 +211,23 @@ def rank_program(g, core, T, topo):
         eb = _bits(_common_mask(topo, core, pair))
         per = len(eb) // 4
         for half, (lsem, rsem) in enumerate(((S.psa, S.rsa), (S.psb, S.rsb))):
-            g.wait_ge(lsem, 32)
+            g.wait_ge(lsem, half_in)
             trs = []
             for qi in range(2):
                 q = 2 * half + qi
                 for w, c in enumerate(pair):
                     mk = _mask(eb[2 * per * qi + w:2 * per * (qi + 1):2])
                     trs.append(RemoteDMATransfer(dst_ids=[_dst(topo, c)], dma_engine_mask=mk, remote_sem=rsem,
-                                                 src=T.tab[BLK * q:BLK * (q + 1), :], dst=T.ptab[BLK * q:BLK * (q + 1), :]))
+                                                 src=T.win[:, TW * q:TW * (q + 1)], dst=T.win[:, TW * q:TW * (q + 1)]))
                     sent += per
             g.remote_dma_fused(trs, local_sem=S.sent)
 
-        g.dma_start(T.lrow[0:1, 0:NPG], T.pt[:, :]).then_inc(S.gl, 16)
-        g.iota(T.ki[:, 0:1], [[0, 1]], 0, 1).then_inc(S.gi, 1)
+        iotas()
         g.iota(T.cm[:, :], [[-1, 2], [-16, 2], [1, NPG]], 0, 0).then_inc(S.gi, 1)
         g.wait_ge(S.gl, 16)
         g.partition_broadcast(T.lb[:, 0:NPG], T.lrow[0:1, 0:NPG], 128).then_inc(S.gb, 1)
 
+        op(vec.memset(T.ones[:, :], 1.0))
         partition_consts()
         bar()
         op(vec.tensor_scalar(T.ma[:, :], T.cm[:, :], T.kf[:, 2:3], 0.0, op0=A.subtract, op1=A.is_equal))
@@ -238,24 +273,27 @@ def rank_program(g, core, T, topo):
         bar()
         op(vec.tensor_tensor(T.kf[:, 16:20], T.kf[:, 16:20], T.kf[:, 12:16], A.add))
         bar()
-        op(vec.tensor_scalar(T.idx[:, 0:4], T.kf[:, 16:20], T.kf[:, 1:2], None, op0=A.add))
+        op(vec.tensor_scalar(T.kf[:, 36:40], T.kf[:, 16:20], 4.0, T.kf[:, 3:4], op0=A.mult, op1=A.add))
+        offsets(36, 4)
 
-        g.wait_ge(S.v, nv[0])
         need = 0
         for s in range(n):
             if s != rank:
                 need += len(_bits(topo.mask(where[(s, rank)][0], core)))
-        g.wait_ge(S.arr, need)
-        rows = T.tab.shape[0]
+        for q in (vec, g.scalar):
+            q.wait_ge(S.v, nv[0])
+            q.wait_ge(S.psa, half_in)
+            q.wait_ge(S.psb, half_in)
+            q.wait_ge(S.arr, need)
         for t in range(4):
-            g.indirect_dma_start(T.tile[:, TW * t:TW * (t + 1)], None, T.tab[:],
-                                 IndirectOffsetOnAxis(ap=T.idx[:, t:t + 1], axis=0), bounds_check=rows - 1).then_inc(gs[t], 16)
-        for t in range(4):
+            pick(t, T.win.shape[1])
+        for t in (0, 2, 1, 3):
             eng = g.sync if t % 2 == 0 else g.scalar
-            eng.wait_ge(gs[t], 16)
-            eng.dma_start(T.y[1024 * t:1024 * (t + 1), :], T.tile[:, TW * t:TW * (t + 1)]).then_inc(S.st, 16)
+            eng.wait_ge(gs[t], 1)
+            for e in range(CAP * t, CAP * (t + 1)):
+                eng.dma_start(T.y[128 * e:128 * (e + 1), :], T.tile[:, PW * e:PW * (e + 1)]).then_inc(S.st, 16)
         g.wait_ge(S.sent, sent)
-        g.wait_ge(S.st, 64)
+        g.wait_ge(S.st, 16 * NPG)
         return
 
     who = [(s, h) for s in range(n) for h in range(NSV) if sv[s][h] == core]
@@ -266,7 +304,7 @@ def rank_program(g, core, T, topo):
     m = len(askers)
     F = NPG * m
     sent = 0
-    g.iota(T.ki[:, 0:1], [[0, 1]], 0, 1).then_inc(S.gi, 1)
+    iotas()
     g.iota(T.cm[:, 0:F], [[0, m], [1, NPG]], 0, 0).then_inc(S.gi, 1)
 
     tg = passon[s][h]
@@ -279,16 +317,16 @@ def rank_program(g, core, T, topo):
 
     pe = _bits(topo.mask(sv[s][h % 2], sv[s][2 + h % 2]))
     hp = len(pe) // 2
+    rper = len(_bits(_common_mask(topo, cores[s], sv[s][0:2]))) // 4
     if h < 2:
-        rper = len(_bits(_common_mask(topo, cores[s], sv[s][0:2]))) // 4
         for half, rsem in enumerate((S.rsa, S.rsb)):
             g.wait_ge(rsem, 2 * rper)
             trs = []
             for qi in range(2):
                 q = 2 * half + qi
                 trs.append(RemoteDMATransfer(dst_ids=[_dst(topo, sv[s][2 + h])], dma_engine_mask=_mask(pe[hp * qi:hp * (qi + 1)]),
-                                             remote_sem=S.rs, src=T.ptab[BLK * q:BLK * (q + 1), :],
-                                             dst=T.ptab[BLK * q:BLK * (q + 1), :]))
+                                             remote_sem=S.rs, src=T.win[:, TW * q:TW * (q + 1)],
+                                             dst=T.win[:, TW * q:TW * (q + 1)]))
                 sent += hp
             g.remote_dma_fused(trs, local_sem=S.sent)
 
@@ -302,18 +340,19 @@ def rank_program(g, core, T, topo):
     g.sync.wait_ge(S.ls, need)
     g.sync.dma_start(T.lrow[0:1, 0:F], T.lists[0:m, 0:16, :]).then_inc(S.sl, 16)
 
-    op(vec.memset(T.ones[0:1, :], 1.0))
+    op(vec.memset(T.ones[:, :], 1.0))
     partition_consts()
     op(vec.tensor_scalar(T.ma[:, 0:F], T.cm[:, 0:F], 0.0, None, op0=A.is_gt))
     vec.wait_ge(S.sl, 16)
     op(vec.tensor_copy(T.lrf[0:1, 0:F], T.lrow[0:1, 0:F]))
     g.tensor.wait_ge(S.v, nv[0])
     g.tensor.matmul(T.pb[:, 0:F], T.ones[0:1, :], T.lrf[0:1, 0:F], True, True).then_inc(S.mm, 1)
-    vec.wait_ge(S.mm, 1)
+    nmm[0] += 1
+    vec.wait_ge(S.mm, nmm[0])
     bar()
     lo = float(NPG * s)
     op(vec.tensor_scalar(T.w4[:, 0:F], T.pb[:, 0:F], lo, lo + float(NPG - 1), op0=A.max, op1=A.min))
-    op(vec.tensor_scalar(T.w3[:, 0:F], T.pb[:, 0:F], lo, float(RPP), op0=A.subtract, op1=A.mult))
+    op(vec.tensor_scalar(T.w3[:, 0:F], T.pb[:, 0:F], lo, float(PW), op0=A.subtract, op1=A.mult))
     bar()
     op(vec.tensor_tensor(T.w0[:, 0:F], T.w4[:, 0:F], T.pb[:, 0:F], A.is_equal))
     bar()
@@ -327,31 +366,26 @@ def rank_program(g, core, T, topo):
     for a in range(m):
         op(vec.tensor_reduce(T.kf[:, 4 + a:5 + a], T.w2[:, NPG * a:NPG * (a + 1)], AxisListType.X, A.add))
     bar()
-    op(vec.tensor_scalar(T.idx[:, 0:m], T.kf[:, 4:4 + m], T.kf[:, 1:2], None, op0=A.add))
+    op(vec.tensor_scalar(T.kf[:, 12:12 + m], T.kf[:, 4:4 + m], T.kf[:, 3:4], None, op0=A.add))
+    offsets(12, m)
 
-    g.wait_ge(S.v, nv[0])
-    if h >= 2:
-        g.wait_ge(S.rs, 4 * hp)
+    for q in (vec, g.scalar):
+        q.wait_ge(S.v, nv[0])
+        if h < 2:
+            q.wait_ge(S.rsa, 2 * rper)
+            q.wait_ge(S.rsb, 2 * rper)
+        else:
+            q.wait_ge(S.rs, 4 * hp)
+    for a in range(m):
+        pick(a, POOLC)
 
-    def gather(a):
-        g.indirect_dma_start(T.tile[:, TW * a:TW * (a + 1)], None, T.ptab[:],
-                             IndirectOffsetOnAxis(ap=T.idx[:, a:a + 1], axis=0), bounds_check=POOLR - 1).then_inc(gs[a], 16)
-
-    def send(a):
+    for a in range(m):
         r = askers[a]
-        base = POOLR + BLK * (s if s < r else s - 1)
+        base = POOLC + TW * (s if s < r else s - 1)
         dst = cores[r]
         rid, pid, _se = topo.addr(dst)
         mk = topo.mask(core, dst)
-        g.wait_ge(gs[a], 16)
-        g.remote_dma(T.tab[base:base + BLK, :], T.tile[:, TW * a:TW * (a + 1)], S.arr, S.sent, pid, rid, mk)
-        return len(_bits(mk))
-
-    ahead = 2 if h < 2 else m
-    for a in range(min(ahead, m)):
-        gather(a)
-    for a in range(m):
-        sent += send(a)
-        if a + ahead < m:
-            gather(a + ahead)
+        g.wait_ge(gs[a], 1)
+        g.remote_dma(T.win[:, base:base + TW], T.tile[:, TW * a:TW * (a + 1)], S.arr, S.sent, pid, rid, mk)
+        sent += len(_bits(mk))
     g.wait_ge(S.sent, sent)

@@ -12,6 +12,8 @@ POOLC = NPG * PW
 OC = 32
 NSV = 4
 MAXD = 4
+NQ = 4
+NF = 8
 
 SCRATCH = {
     "win": ("sbuf", [128, POOLC + 11 * TW], "float32"),
@@ -43,8 +45,8 @@ SCRATCH = {
     "ki": ("sbuf", [128, 16], "int32"),
     "kf": ("sbuf", [128, 40], "float32"),
 }
-SEMAPHORES = ["ms", "psa", "psb", "gl", "sl", "mm", "gs0", "gs1", "gs2", "gs3", "gi", "gb", "v", "fs", "ls",
-              "rsa", "rsb", "rs", "arr", "sent", "st", "zs"]
+SEMAPHORES = ["ms", "ps0", "ps1", "ps2", "ps3", "gl", "sl", "mm", "gs0", "gs1", "gs2", "gs3", "gs4", "gs5", "gs6", "gs7",
+              "gi", "gb", "v", "fs", "ls", "rq0", "rq1", "rq2", "rq3", "rs", "arr", "sent", "st", "zs", "lsn"]
 
 
 def _bits(mask):
@@ -136,6 +138,8 @@ def rank_program(g, core, T, topo):
     vec = g.vector
     nv = [0]
     nmm = [0]
+    ps = [S.ps0, S.ps1, S.ps2, S.ps3]
+    rq = [S.rq0, S.rq1, S.rq2, S.rq3]
 
     def bar():
         if nv[0]:
@@ -171,14 +175,14 @@ def rank_program(g, core, T, topo):
         vec.wait_ge(S.mm, nmm[0])
         op(vec.tensor_scalar(T.off[:, 0:OC * m], T.pb2[:, 0:OC * m], T.kf[:, 1:2], None, op0=A.add))
 
-    gs = [S.gs0, S.gs1, S.gs2, S.gs3]
+    gs = [S.gs0, S.gs1, S.gs2, S.gs3, S.gs4, S.gs5, S.gs6, S.gs7]
 
-    def pick(a, cols):
-        src = T.win[:, 0:cols].indirect(T.off[:, OC * a:OC * (a + 1)])
+    def pick(a, cols, oc):
+        src = T.win[:, 0:cols].indirect(T.off[:, oc * a:oc * (a + 1)])
         if a % 2 == 0:
-            vec.tensor_copy(T.tile[:, TW * a:TW * (a + 1)], src).then_inc(gs[a], 1)
+            vec.tensor_copy(T.tile[:, 16 * oc * a:16 * oc * (a + 1)], src).then_inc(gs[a], 1)
         else:
-            g.scalar.activation(T.tile[:, TW * a:TW * (a + 1)], src, ActivationFunctionType.Copy).then_inc(gs[a], 1)
+            g.scalar.activation(T.tile[:, 16 * oc * a:16 * oc * (a + 1)], src, ActivationFunctionType.Copy).then_inc(gs[a], 1)
 
     rank = T.rank_of(core)
 
@@ -190,36 +194,33 @@ def rank_program(g, core, T, topo):
         vec.memset(T.zr[0:1, :], 0).then_inc(S.zs, 1)
         g.scalar.wait_ge(S.zs, 1)
         g.scalar.dma_start(T.mylist[16:128, :], T.zr[0:1, :]).then_inc(S.ms, 16)
+        ppq = NPG // NQ
         for pg in range(NPG):
+            if pg == NPG // 2:
+                g.sync.wait_ge(S.lsn, 2)
+                g.scalar.wait_ge(S.lsn, 2)
             eng = g.scalar if pg % 2 == 0 else g.sync
-            eng.dma_start(T.win[:, PW * pg:PW * (pg + 1)], T.pool[128 * pg:128 * (pg + 1), :]).then_inc(
-                S.psa if pg < NPG // 2 else S.psb, 16)
-        half_in = 16 * (NPG // 2)
+            eng.dma_start(T.win[:, PW * pg:PW * (pg + 1)], T.pool[128 * pg:128 * (pg + 1), :]).then_inc(ps[pg // ppq], 16)
+        q_in = 16 * ppq
 
         g.wait_ge(S.ms, 32)
         dg = direct[rank]
         lm = _mask(_bits(_common_mask(topo, core, mine + [c for c, a in dg]))[:1])
         g.remote_dma_fused([RemoteDMATransfer(dst_ids=[_dst(topo, c) for c in mine], dma_engine_mask=lm, remote_sem=S.fs,
                                               srcs=[T.mylist[:, :]], dsts=[T.fwd[:, :] for c in mine], alu_op=0)],
-                           local_sem=S.sent)
-        sent += 1
+                           local_sem=S.lsn)
         g.remote_dma_fused([RemoteDMATransfer(dst_ids=[_dst(topo, c) for c, a in dg], dma_engine_mask=lm, remote_sem=S.ls,
                                               srcs=[T.mylist[:, :]], dsts=[T.lists[a] for c, a in dg], alu_op=0)],
-                           local_sem=S.sent)
-        sent += 1
+                           local_sem=S.lsn)
         pair = mine[0:2]
         eb = _bits(_common_mask(topo, core, pair))
-        per = len(eb) // 4
-        for half, (lsem, rsem) in enumerate(((S.psa, S.rsa), (S.psb, S.rsb))):
-            g.wait_ge(lsem, half_in)
+        for q in range(NQ):
+            g.wait_ge(ps[q], q_in)
             trs = []
-            for qi in range(2):
-                q = 2 * half + qi
-                for w, c in enumerate(pair):
-                    mk = _mask(eb[2 * per * qi + w:2 * per * (qi + 1):2])
-                    trs.append(RemoteDMATransfer(dst_ids=[_dst(topo, c)], dma_engine_mask=mk, remote_sem=rsem,
-                                                 src=T.win[:, TW * q:TW * (q + 1)], dst=T.win[:, TW * q:TW * (q + 1)]))
-                    sent += per
+            for w, c in enumerate(pair):
+                trs.append(RemoteDMATransfer(dst_ids=[_dst(topo, c)], dma_engine_mask=_mask(eb[w::2]), remote_sem=rq[q],
+                                             src=T.win[:, TW * q:TW * (q + 1)], dst=T.win[:, TW * q:TW * (q + 1)]))
+                sent += len(eb[w::2])
             g.remote_dma_fused(trs, local_sem=S.sent)
 
         iotas()
@@ -280,18 +281,28 @@ def rank_program(g, core, T, topo):
         for s in range(n):
             if s != rank:
                 need += len(_bits(topo.mask(where[(s, rank)][0], core)))
-        for q in (vec, g.scalar):
-            q.wait_ge(S.v, nv[0])
-            q.wait_ge(S.psa, half_in)
-            q.wait_ge(S.psb, half_in)
-            q.wait_ge(S.arr, need)
-        for t in range(4):
-            pick(t, T.win.shape[1])
-        for t in (0, 2, 1, 3):
-            eng = g.sync if t % 2 == 0 else g.scalar
-            eng.wait_ge(gs[t], 1)
-            for e in range(CAP * t, CAP * (t + 1)):
+        for qu in (vec, g.scalar):
+            qu.wait_ge(S.v, nv[0])
+            for q in range(NQ):
+                qu.wait_ge(ps[q], q_in)
+            qu.wait_ge(S.arr, need)
+        ppf = NPG // NF
+        foc = 4 * ppf
+        wc = T.win.shape[1]
+
+        def store(eng, u):
+            eng.wait_ge(gs[u], 1)
+            for e in range(ppf * u, ppf * (u + 1)):
                 eng.dma_start(T.y[128 * e:128 * (e + 1), :], T.tile[:, PW * e:PW * (e + 1)]).then_inc(S.st, 16)
+
+        for u in range(0, NF, 2):
+            pick(u, wc, foc)
+            store(g.sync, u)
+        pick(1, wc, foc)
+        for u in range(3, NF, 2):
+            pick(u, wc, foc)
+            store(g.scalar, u - 2)
+        store(g.scalar, NF - 1)
         g.wait_ge(S.sent, sent)
         g.wait_ge(S.st, 16 * NPG)
         return
@@ -315,20 +326,15 @@ def rank_program(g, core, T, topo):
                        local_sem=S.sent)
     sent += len(_bits(fm))
 
-    pe = _bits(topo.mask(sv[s][h % 2], sv[s][2 + h % 2]))
-    hp = len(pe) // 2
-    rper = len(_bits(_common_mask(topo, cores[s], sv[s][0:2]))) // 4
+    pm = topo.mask(sv[s][h % 2], sv[s][2 + h % 2])
+    npe = len(_bits(pm))
+    rper = len(_bits(_common_mask(topo, cores[s], sv[s][0:2]))) // 2
     if h < 2:
-        for half, rsem in enumerate((S.rsa, S.rsb)):
-            g.wait_ge(rsem, 2 * rper)
-            trs = []
-            for qi in range(2):
-                q = 2 * half + qi
-                trs.append(RemoteDMATransfer(dst_ids=[_dst(topo, sv[s][2 + h])], dma_engine_mask=_mask(pe[hp * qi:hp * (qi + 1)]),
-                                             remote_sem=S.rs, src=T.win[:, TW * q:TW * (q + 1)],
-                                             dst=T.win[:, TW * q:TW * (q + 1)]))
-                sent += hp
-            g.remote_dma_fused(trs, local_sem=S.sent)
+        rid2, pid2, _se2 = topo.addr(sv[s][2 + h])
+        for q in range(NQ):
+            g.wait_ge(rq[q], rper)
+            g.remote_dma(T.win[:, TW * q:TW * (q + 1)], T.win[:, TW * q:TW * (q + 1)], S.rs, S.sent, pid2, rid2, pm)
+            sent += npe
 
     need = 0
     for r in askers:
@@ -369,15 +375,15 @@ def rank_program(g, core, T, topo):
     op(vec.tensor_scalar(T.kf[:, 12:12 + m], T.kf[:, 4:4 + m], T.kf[:, 3:4], None, op0=A.add))
     offsets(12, m)
 
-    for q in (vec, g.scalar):
-        q.wait_ge(S.v, nv[0])
+    for qu in (vec, g.scalar):
+        qu.wait_ge(S.v, nv[0])
         if h < 2:
-            q.wait_ge(S.rsa, 2 * rper)
-            q.wait_ge(S.rsb, 2 * rper)
+            for q in range(NQ):
+                qu.wait_ge(rq[q], rper)
         else:
-            q.wait_ge(S.rs, 4 * hp)
+            qu.wait_ge(S.rs, NQ * npe)
     for a in range(m):
-        pick(a, POOLC)
+        pick(a, POOLC, OC)
 
     for a in range(m):
         r = askers[a]

from concourse.bass import DstId, RemoteDMATransfer
from concourse.mybir import AluOpType, AxisListType, ActivationFunctionType

NPG = 32
CAP = 8
PW = 64
RPP = 16
TW = CAP * PW
BLK = 128
POOLR = NPG * RPP
POOLC = NPG * PW
OC = 32
NSV = 4
MAXD = 4
NQ = 4
NF = 8

SCRATCH = {
    "win": ("sbuf", [128, POOLC + 11 * TW], "float32"),
    "tile": ("sbuf", [128, MAXD * TW], "float32"),
    "mylist": ("dram", [128, 2], "int32"),
    "fwd": ("dram", [128, 2], "int32"),
    "lists": ("dram", [MAXD, 128, 2], "int32"),
    "zr": ("sbuf", [128, 224], "int32"),
    "lrow": ("sbuf", [128, 128], "int32"),
    "lrf": ("sbuf", [128, 128], "float32"),
    "ones": ("sbuf", [128, 128], "float32"),
    "pb": ("psum", [128, 128], "float32"),
    "pb2": ("psum", [128, 128], "float32"),
    "lb": ("sbuf", [128, 128], "int32"),
    "cm": ("sbuf", [128, 128], "int32"),
    "dm": ("sbuf", [128, OC], "int32"),
    "dd": ("sbuf", [128, OC], "float32"),
    "rhs": ("sbuf", [128, 128], "float32"),
    "off": ("sbuf", [128, 128], "uint16"),
    "own": ("sbuf", [128, 128], "int32"),
    "ma": ("sbuf", [128, 128], "float32"),
    "mb": ("sbuf", [128, 128], "float32"),
    "w0": ("sbuf", [128, 128], "float32"),
    "w1": ("sbuf", [128, 128], "float32"),
    "w2": ("sbuf", [128, 128], "float32"),
    "w3": ("sbuf", [128, 128], "float32"),
    "w4": ("sbuf", [128, 128], "float32"),
    "w5": ("sbuf", [128, 128], "float32"),
    "ki": ("sbuf", [128, 16], "int32"),
    "kf": ("sbuf", [128, 40], "float32"),
}
SEMAPHORES = ["ms", "ps0", "ps1", "ps2", "ps3", "gl", "sl", "mm", "gs0", "gs1", "gs2", "gs3", "gs4", "gs5", "gs6", "gs7",
              "gi", "gb", "v", "fs", "ls", "rq0", "rq1", "rq2", "rq3", "rs", "arr", "sent", "st", "zs", "lsn"]


def _bits(mask):
    return [b for b in range(mask.bit_length()) if (mask >> b) & 1]


def _mask(bits):
    m = 0
    for b in bits:
        m |= 1 << b
    return m


def _plan(cores, topo):
    n = len(cores)
    allc = range(topo.CHIPS * topo.CORES_PER_CHIP)
    chips = [topo.chip(c) for c in cores]
    mate = {}
    for a in range(topo.CHIPS):
        for b in range(topo.CHIPS):
            if topo.mates(a, b):
                mate[a] = b
    sv = []
    for i, rc in enumerate(cores):
        probe = [c for c in allc if topo.chip(c) == mate[chips[i]]][0]
        ownr = [c for c in allc if topo.chip(c) == chips[i] and c != rc and topo.may_write(c, probe)]
        near = [c for c in ownr if topo.die(c) == topo.die(rc)]
        far = [c for c in ownr if topo.die(c) != topo.die(rc)]
        sv.append([near[0], far[0], near[1], far[1]])

    def links(a, b, d):
        if topo.same_plane(a, b):
            return [("out", a, d), ("in", b, d)]
        if topo.mates(a, b):
            return [("mate", a, d)]
        return [("mate", a, d), ("out", mate[a], d), ("in", b, d)]

    load = {}
    side = {}
    for k in range(1, n):
        for s in range(n):
            r = (s + k) % n
            best = None
            for h in (0, 1):
                d = topo.die(sv[s][h])
                ls = links(chips[s], chips[r], d) + [("src", s, d)]
                key = (max(load.get(x, 0) for x in ls), sum(load.get(x, 0) for x in ls), h)
                if best is None or key < best[0]:
                    best = (key, h, ls)
            for x in best[2]:
                load[x] = load.get(x, 0) + 1
            side[(s, r)] = best[1]
    serve = [[[] for h in range(NSV)] for s in range(n)]
    where = {}
    for s in range(n):
        for h in (0, 1):
            ds = [(s + k) % n for k in range(1, n) if side[(s, (s + k) % n)] == h]
            ds.sort(key=lambda r: 0 if topo.may_write(cores[r], sv[s][h]) else 1)
            late = len(ds) // 2
            serve[s][h] = ds[:len(ds) - late]
            serve[s][2 + h] = ds[len(ds) - late:]
        for h in range(NSV):
            for a, r in enumerate(serve[s][h]):
                where[(s, r)] = (sv[s][h], a)
    direct = [[where[(s, r)] for s in range(n) if s != r and topo.may_write(cores[r], where[(s, r)][0])] for r in range(n)]
    passon = [[[where[(s, r)] for s in [x for x in range(n) if x != r and not topo.may_write(cores[r], where[(x, r)][0])][h::NSV]]
               for h in range(NSV)] for r in range(n)]
    return sv, serve, where, passon, direct


def _common_mask(topo, src, dsts):
    m = topo.mask(src, dsts[0])
    for d in dsts[1:]:
        m &= topo.mask(src, d)
    return m


def _dst(topo, c):
    rid, pid, _se = topo.addr(c)
    return DstId(rid=rid, pnc=pid)


def rank_program(g, core, T, topo):
    cores = list(T.cores)
    n = len(cores)
    sv, serve, where, passon, direct = _plan(cores, topo)
    S = T.sem
    A = AluOpType
    vec = g.vector
    nv = [0]
    nmm = [0]
    ps = [S.ps0, S.ps1, S.ps2, S.ps3]
    rq = [S.rq0, S.rq1, S.rq2, S.rq3]

    def bar():
        if nv[0]:
            vec.wait_ge(S.v, nv[0])

    def op(ins):
        ins.then_inc(S.v, 1)
        nv[0] += 1

    def iotas():
        g.iota(T.ki[:, 0:1], [[0, 1]], 0, 1).then_inc(S.gi, 1)
        g.iota(T.dm[:, :], [[16, CAP], [1, 4]], 0, -1).then_inc(S.gi, 1)

    def partition_consts():
        vec.wait_ge(S.gi, 3)
        op(vec.tensor_scalar(T.ki[:, 1:2], T.ki[:, 0:1], 4, None, op0=A.arith_shift_right))
        op(vec.tensor_scalar(T.ki[:, 2:3], T.ki[:, 0:1], 15, None, op0=A.bitwise_and))
        op(vec.tensor_scalar(T.ki[:, 3:4], T.ki[:, 0:1], 3, None, op0=A.bitwise_and))
        op(vec.tensor_scalar(T.dd[:, :], T.dm[:, :], 0.0, None, op0=A.is_equal))
        bar()
        op(vec.tensor_scalar(T.kf[:, 0:1], T.ki[:, 1:2], 1.0, None, op0=A.add))
        op(vec.tensor_copy(T.kf[:, 1:2], T.ki[:, 2:3]))
        op(vec.tensor_scalar(T.kf[:, 2:3], T.ki[:, 1:2], 2.0, None, op0=A.mult))
        op(vec.tensor_scalar(T.kf[:, 3:4], T.ki[:, 3:4], 16.0, None, op0=A.mult))

    def offsets(v0, m):
        bar()
        for a in range(m):
            op(vec.tensor_scalar(T.rhs[:, OC * a:OC * (a + 1)], T.dd[:, :], T.kf[:, v0 + a:v0 + a + 1], None, op0=A.mult))
        g.tensor.wait_ge(S.v, nv[0])
        g.tensor.matmul(T.pb2[:, 0:OC * m], T.ones[:, :], T.rhs[:, 0:OC * m], True, True).then_inc(S.mm, 1)
        nmm[0] += 1
        vec.wait_ge(S.mm, nmm[0])
        op(vec.tensor_scalar(T.off[:, 0:OC * m], T.pb2[:, 0:OC * m], T.kf[:, 1:2], None, op0=A.add))

    gs = [S.gs0, S.gs1, S.gs2, S.gs3, S.gs4, S.gs5, S.gs6, S.gs7]

    def pick(a, cols, oc):
        src = T.win[:, 0:cols].indirect(T.off[:, oc * a:oc * (a + 1)])
        if a % 2 == 0:
            vec.tensor_copy(T.tile[:, 16 * oc * a:16 * oc * (a + 1)], src).then_inc(gs[a], 1)
        else:
            g.scalar.activation(T.tile[:, 16 * oc * a:16 * oc * (a + 1)], src, ActivationFunctionType.Copy).then_inc(gs[a], 1)

    rank = T.rank_of(core)

    if rank is not None:
        mine = sv[rank]
        sent = 0
        g.sync.dma_start(T.mylist[0:16, :], T.pt[:, :]).then_inc(S.ms, 16)
        g.sync.dma_start(T.lrow[0:1, 0:NPG], T.pt[:, :]).then_inc(S.gl, 16)
        vec.memset(T.zr[0:1, :], 0).then_inc(S.zs, 1)
        g.scalar.wait_ge(S.zs, 1)
        g.scalar.dma_start(T.mylist[16:128, :], T.zr[0:1, :]).then_inc(S.ms, 16)
        ppq = NPG // NQ
        for pg in range(NPG):
            if pg == NPG // 2:
                g.sync.wait_ge(S.lsn, 2)
                g.scalar.wait_ge(S.lsn, 2)
            eng = g.scalar if pg % 2 == 0 else g.sync
            eng.dma_start(T.win[:, PW * pg:PW * (pg + 1)], T.pool[128 * pg:128 * (pg + 1), :]).then_inc(ps[pg // ppq], 16)
        q_in = 16 * ppq

        g.wait_ge(S.ms, 32)
        dg = direct[rank]
        lm = _mask(_bits(_common_mask(topo, core, mine + [c for c, a in dg]))[:1])
        g.remote_dma_fused([RemoteDMATransfer(dst_ids=[_dst(topo, c) for c in mine], dma_engine_mask=lm, remote_sem=S.fs,
                                              srcs=[T.mylist[:, :]], dsts=[T.fwd[:, :] for c in mine], alu_op=0)],
                           local_sem=S.lsn)
        g.remote_dma_fused([RemoteDMATransfer(dst_ids=[_dst(topo, c) for c, a in dg], dma_engine_mask=lm, remote_sem=S.ls,
                                              srcs=[T.mylist[:, :]], dsts=[T.lists[a] for c, a in dg], alu_op=0)],
                           local_sem=S.lsn)
        pair = mine[0:2]
        eb = _bits(_common_mask(topo, core, pair))
        for q in range(NQ):
            g.wait_ge(ps[q], q_in)
            trs = []
            for w, c in enumerate(pair):
                trs.append(RemoteDMATransfer(dst_ids=[_dst(topo, c)], dma_engine_mask=_mask(eb[w::2]), remote_sem=rq[q],
                                             src=T.win[:, TW * q:TW * (q + 1)], dst=T.win[:, TW * q:TW * (q + 1)]))
                sent += len(eb[w::2])
            g.remote_dma_fused(trs, local_sem=S.sent)

        iotas()
        g.iota(T.cm[:, :], [[-1, 2], [-16, 2], [1, NPG]], 0, 0).then_inc(S.gi, 1)
        g.wait_ge(S.gl, 16)
        g.partition_broadcast(T.lb[:, 0:NPG], T.lrow[0:1, 0:NPG], 128).then_inc(S.gb, 1)

        op(vec.memset(T.ones[:, :], 1.0))
        partition_consts()
        bar()
        op(vec.tensor_scalar(T.ma[:, :], T.cm[:, :], T.kf[:, 2:3], 0.0, op0=A.subtract, op1=A.is_equal))
        op(vec.tensor_scalar(T.mb[:, :], T.cm[:, :], T.kf[:, 2:3], 0.0, op0=A.subtract, op1=A.is_lt))
        vec.wait_ge(S.gb, 1)
        op(vec.tensor_copy(T.w0[:, 0:NPG], T.lb[:, 0:NPG]))
        op(vec.tensor_scalar(T.own[:, 0:NPG], T.lb[:, 0:NPG], 5, None, op0=A.arith_shift_right))
        bar()
        op(vec.tensor_copy(T.w1[:, 0:NPG], T.own[:, 0:NPG]))
        for t in range(4):
            op(vec.tensor_tensor(T.w2[:, NPG * t:NPG * (t + 1)], T.ma[:, NPG * t:NPG * (t + 1)], T.w0[:, 0:NPG], A.mult))
        bar()
        for t in range(4):
            op(vec.tensor_reduce(T.kf[:, 4 + t:5 + t], T.w2[:, NPG * t:NPG * (t + 1)], AxisListType.X, A.add))
        bar()
        op(vec.tensor_copy(T.ki[:, 4:8], T.kf[:, 4:8]))
        bar()
        op(vec.tensor_scalar(T.ki[:, 8:12], T.ki[:, 4:8], 5, None, op0=A.arith_shift_right))
        op(vec.tensor_scalar(T.ki[:, 12:16], T.ki[:, 4:8], NPG - 1, None, op0=A.bitwise_and))
        bar()
        op(vec.tensor_copy(T.kf[:, 8:12], T.ki[:, 8:12]))
        op(vec.tensor_scalar(T.kf[:, 12:16], T.ki[:, 12:16], float(RPP), None, op0=A.mult))
        bar()
        for t in range(4):
            op(vec.tensor_scalar(T.w3[:, NPG * t:NPG * (t + 1)], T.w1[:, 0:NPG], T.kf[:, 8 + t:9 + t], None, op0=A.is_equal))
        op(vec.tensor_scalar(T.kf[:, 16:20], T.kf[:, 8:12], float(BLK), float(POOLR), op0=A.mult, op1=A.add))
        op(vec.tensor_scalar(T.kf[:, 20:24], T.kf[:, 8:12], float(rank), None, op0=A.is_equal))
        op(vec.tensor_scalar(T.kf[:, 32:36], T.kf[:, 8:12], float(rank), float(BLK), op0=A.is_gt, op1=A.mult))
        bar()
        op(vec.tensor_tensor(T.w2[:, :], T.w3[:, :], T.mb[:, :], A.mult))
        bar()
        for t in range(4):
            op(vec.tensor_reduce(T.kf[:, 24 + t:25 + t], T.w2[:, NPG * t:NPG * (t + 1)], AxisListType.X, A.add))
        bar()
        op(vec.tensor_scalar(T.kf[:, 28:32], T.kf[:, 24:28], float(RPP), None, op0=A.mult))
        op(vec.tensor_tensor(T.kf[:, 16:20], T.kf[:, 16:20], T.kf[:, 32:36], A.subtract))
        bar()
        op(vec.tensor_tensor(T.kf[:, 16:20], T.kf[:, 16:20], T.kf[:, 28:32], A.add))
        bar()
        op(vec.tensor_tensor(T.kf[:, 12:16], T.kf[:, 12:16], T.kf[:, 16:20], A.subtract))
        bar()
        op(vec.tensor_tensor(T.kf[:, 12:16], T.kf[:, 12:16], T.kf[:, 20:24], A.mult))
        bar()
        op(vec.tensor_tensor(T.kf[:, 16:20], T.kf[:, 16:20], T.kf[:, 12:16], A.add))
        bar()
        op(vec.tensor_scalar(T.kf[:, 36:40], T.kf[:, 16:20], 4.0, T.kf[:, 3:4], op0=A.mult, op1=A.add))
        offsets(36, 4)

        need = 0
        for s in range(n):
            if s != rank:
                need += len(_bits(topo.mask(where[(s, rank)][0], core)))
        for qu in (vec, g.scalar):
            qu.wait_ge(S.v, nv[0])
            for q in range(NQ):
                qu.wait_ge(ps[q], q_in)
            qu.wait_ge(S.arr, need)
        ppf = NPG // NF
        foc = 4 * ppf
        wc = T.win.shape[1]

        def store(eng, u):
            eng.wait_ge(gs[u], 1)
            for e in range(ppf * u, ppf * (u + 1)):
                eng.dma_start(T.y[128 * e:128 * (e + 1), :], T.tile[:, PW * e:PW * (e + 1)]).then_inc(S.st, 16)

        for u in range(0, NF, 2):
            pick(u, wc, foc)
            store(g.sync, u)
        pick(1, wc, foc)
        for u in range(3, NF, 2):
            pick(u, wc, foc)
            store(g.scalar, u - 2)
        store(g.scalar, NF - 1)
        g.wait_ge(S.sent, sent)
        g.wait_ge(S.st, 16 * NPG)
        return

    who = [(s, h) for s in range(n) for h in range(NSV) if sv[s][h] == core]
    if not who:
        return
    s, h = who[0]
    askers = serve[s][h]
    m = len(askers)
    F = NPG * m
    sent = 0
    iotas()
    g.iota(T.cm[:, 0:F], [[0, m], [1, NPG]], 0, 0).then_inc(S.gi, 1)

    tg = passon[s][h]
    fm = _common_mask(topo, core, [c for c, a in tg])
    g.wait_ge(S.fs, 1)
    g.remote_dma_fused([RemoteDMATransfer(dst_ids=[_dst(topo, c) for c, a in tg], dma_engine_mask=fm, remote_sem=S.ls,
                                          srcs=[T.fwd[:, :]], dsts=[T.lists[a] for c, a in tg], alu_op=0)],
                       local_sem=S.sent)
    sent += len(_bits(fm))

    pm = topo.mask(sv[s][h % 2], sv[s][2 + h % 2])
    npe = len(_bits(pm))
    rper = len(_bits(_common_mask(topo, cores[s], sv[s][0:2]))) // 2
    if h < 2:
        rid2, pid2, _se2 = topo.addr(sv[s][2 + h])
        for q in range(NQ):
            g.wait_ge(rq[q], rper)
            g.remote_dma(T.win[:, TW * q:TW * (q + 1)], T.win[:, TW * q:TW * (q + 1)], S.rs, S.sent, pid2, rid2, pm)
            sent += npe

    need = 0
    for r in askers:
        if (core, askers.index(r)) in direct[r]:
            need += 1
        for hh in range(NSV):
            if (core, askers.index(r)) in passon[r][hh]:
                need += len(_bits(_common_mask(topo, sv[r][hh], [c for c, a in passon[r][hh]])))
    g.sync.wait_ge(S.ls, need)
    g.sync.dma_start(T.lrow[0:1, 0:F], T.lists[0:m, 0:16, :]).then_inc(S.sl, 16)

    op(vec.memset(T.ones[:, :], 1.0))
    partition_consts()
    op(vec.tensor_scalar(T.ma[:, 0:F], T.cm[:, 0:F], 0.0, None, op0=A.is_gt))
    vec.wait_ge(S.sl, 16)
    op(vec.tensor_copy(T.lrf[0:1, 0:F], T.lrow[0:1, 0:F]))
    g.tensor.wait_ge(S.v, nv[0])
    g.tensor.matmul(T.pb[:, 0:F], T.ones[0:1, :], T.lrf[0:1, 0:F], True, True).then_inc(S.mm, 1)
    nmm[0] += 1
    vec.wait_ge(S.mm, nmm[0])
    bar()
    lo = float(NPG * s)
    op(vec.tensor_scalar(T.w4[:, 0:F], T.pb[:, 0:F], lo, lo + float(NPG - 1), op0=A.max, op1=A.min))
    op(vec.tensor_scalar(T.w3[:, 0:F], T.pb[:, 0:F], lo, float(PW), op0=A.subtract, op1=A.mult))
    bar()
    op(vec.tensor_tensor(T.w0[:, 0:F], T.w4[:, 0:F], T.pb[:, 0:F], A.is_equal))
    bar()
    op(vec.tensor_tensor_scan(T.w1[:, 0:F], T.ma[:, 0:F], T.w0[:, 0:F], 0.0, A.mult, A.add))
    op(vec.tensor_tensor(T.w5[:, 0:F], T.w0[:, 0:F], T.w3[:, 0:F], A.mult))
    bar()
    op(vec.tensor_scalar(T.mb[:, 0:F], T.w1[:, 0:F], T.kf[:, 0:1], None, op0=A.is_equal))
    bar()
    op(vec.tensor_tensor(T.w2[:, 0:F], T.mb[:, 0:F], T.w5[:, 0:F], A.mult))
    bar()
    for a in range(m):
        op(vec.tensor_reduce(T.kf[:, 4 + a:5 + a], T.w2[:, NPG * a:NPG * (a + 1)], AxisListType.X, A.add))
    bar()
    op(vec.tensor_scalar(T.kf[:, 12:12 + m], T.kf[:, 4:4 + m], T.kf[:, 3:4], None, op0=A.add))
    offsets(12, m)

    for qu in (vec, g.scalar):
        qu.wait_ge(S.v, nv[0])
        if h < 2:
            for q in range(NQ):
                qu.wait_ge(rq[q], rper)
        else:
            qu.wait_ge(S.rs, NQ * npe)
    for a in range(m):
        pick(a, POOLC, OC)

    for a in range(m):
        r = askers[a]
        base = POOLC + TW * (s if s < r else s - 1)
        dst = cores[r]
        rid, pid, _se = topo.addr(dst)
        mk = topo.mask(core, dst)
        g.wait_ge(gs[a], 1)
        g.remote_dma(T.win[:, base:base + TW], T.tile[:, TW * a:TW * (a + 1)], S.arr, S.sent, pid, rid, mk)
        sent += len(_bits(mk))
    g.wait_ge(S.sent, sent)
